import numpy as np, ml_dtypes
CORES = [1,5,17,21,33,37,49,53]
N = 8
BF = ml_dtypes.bfloat16
VX, VY, C, B, LE = 2048, 4096, 256, 2, 5
def parts(rng):
    X = rng.integers(0, 256, (N, 8, 16, VX)); Y = rng.integers(0, 256, (N, 8, 16, VY))
    K = rng.integers(0, VX, (N, 8, 16, C)); G = rng.integers(0, VY, (N, 8, 16, B * C)); W = rng.integers(0, VX, (N, 8, 16, B * C))
    z = rng.integers(0, 256, (N, 8, 16, C)); w = rng.integers(0, 64, (N, 8, 16, 1)); t = rng.integers(1000, 1451, (N, 8, 16, 1))
    return X, Y, K, G, W, z, w, t
def pack(X, Y, K, G, W, z, w, t):
    fl = lambda a: np.ascontiguousarray(np.reshape(a, (N, 128, -1))).astype(np.float32).astype(BF)
    wh = lambda a: np.ascontiguousarray(np.reshape(a, (N, 128, -1))).astype(np.int32)
    return {"gx": fl(X), "sy": fl(Y), "rk": wh(K), "rt": wh(G), "wr": wh(W), "z0": fl(z), "wt": fl(w), "th": wh(t)}
def setup_inputs(rng):
    return pack(*parts(rng))
def uneven(rng, top, bits, shape):
    v = np.exp2(bits * rng.random(shape)).astype(np.int64) - 1
    return np.minimum(np.maximum(np.where(rng.random(shape) < 0.5, v, top - v), 0), top)
def setup_inputs_spread(rng):
    X, Y, K, G, W, z, w, t = parts(rng)
    X = (np.exp2(8 * rng.random((N, 8, 1, VX))) * rng.random(X.shape)).astype(np.int64)
    Y = (np.exp2(8 * rng.random((N, 8, 1, VY))) * rng.random(Y.shape)).astype(np.int64)
    z = (np.exp2(8 * rng.random((N, 8, 1, C))) * rng.random(z.shape)).astype(np.int64)
    lx = VX.bit_length() - 1; ly = VY.bit_length() - 1
    K = uneven(rng, VX - 1, lx, K.shape); W = uneven(rng, VX - 1, lx, W.shape); G = uneven(rng, VY - 1, ly, G.shape)
    w = uneven(rng, 63, 6, w.shape); t = rng.integers(0, 4081, t.shape)
    return pack(X, Y, K, G, W, z, w, t)
def setup_inputs_ends(rng):
    sh = np.array([0.0, 0.1, 0.5, 0.9, 1.0])
    X = 255 * (rng.random((N, 8, 16, VX)) < rng.choice(sh, (N, 8, 1, VX))); Y = 255 * (rng.random((N, 8, 16, VY)) < rng.choice(sh, (N, 8, 1, VY)))
    K = (VX - 1) * rng.integers(0, 2, (N, 8, 16, C)); G = (VY - 1) * rng.integers(0, 2, (N, 8, 16, B * C)); W = (VX - 1) * rng.integers(0, 2, (N, 8, 16, B * C))
    z = 255 * rng.integers(0, 2, (N, 8, 16, C)); w = 63 * rng.integers(0, 2, (N, 8, 16, 1)); t = 4080 * (rng.random((N, 8, 16, 1)) < 0.75)
    w[:, :, 0] = 63; w[:, 0, 1] = 0; t[:, 0] = 4080; t[:, 3, :4] = 0
    for q in range(N):
        for g in range(7):
            m = (q + g) % 4
            if m == 0: X[q, g, :, 0] = 0; X[q, g, :, VX - 1] = 255
            if m == 1: X[q, g, :, 0] = 255; X[q, g, :, VX - 1] = 0
            if m == 2: X[q, g, :, 0] = 255 * rng.integers(0, 2, 16); X[q, g, :, VX - 1] = 255
            if m == 3: X[q, g, :, 0] = 255 * rng.integers(0, 2, 16); X[q, g, :, VX - 1] = 255 * rng.integers(0, 2, 16)
    m1 = [m for m in range(1, 17) if (((((255 * 63 * m) & 4095) ** 2) >> 5) & (B - 1)) == B - 1][0]
    s1 = (VY - 1 + 37 * ((255 * 63 * m1) & 4095)) & (VY - 1)
    X[:, 7, :, 0] = 0; X[:, 7, :, VX - 1] = 255; Y[:, 7, :, 0] = 0; Y[:, 7, :, VY - 1] = 255; Y[:, 7, :, s1] = 255; w[:, 7] = 63; t[:, 7] = 4080
    for i, m in ((C - 1, m1), (C - 2, 0), (C - 3, 13), (C - 4, 16), (0, m1), (1, 0), (2, 16)):
        z[:, 7, :, i] = 255 * (np.arange(16) < m)
        K[:, 7, 15, i] = 0; K[:, 7, 14, i] = VX - 1; K[:, 7, 0, i] = 0; G[:, 7, 14:, B * i:B * i + B] = VY - 1; G[:, 7, 0, B * i:B * i + B] = VY - 1
    return pack(X, Y, K, G, W, z, w, t)
def setup_inputs_corners(rng):
    X, Y, K, G, W, z, w, t = parts(rng); h = VX // 2; v = VY // 4
    X[..., :h] = rng.integers(0, 48, (N, 8, 16, h)); X[..., h:] = rng.integers(208, 256, (N, 8, 16, VX - h)); Y[..., :v] = rng.integers(0, 48, (N, 8, 16, v))
    kind = rng.integers(0, 8, (N, 8, 1, C)); kind[..., :8] = np.arange(8); kind[..., C - 8:] = np.arange(8)
    k = np.arange(16)[:, None]; lane = rng.integers(0, 16, (N, 8, 1, C))
    up = ((kind == 1) & (k == 0)) | ((kind == 2) & (k == 15)) | ((kind == 3) & (k == lane)) | ((kind == 4) & (k <= lane))
    lh = np.where(up, rng.integers(h, VX, K.shape), rng.integers(0, h, K.shape))
    K = np.where(kind == 7, (VX - 1) * rng.integers(0, 2, K.shape), np.where(kind == 6, K, lh))
    z = np.where(kind < 5, rng.integers(64, 96, z.shape), np.where(kind == 5, 255, np.where(kind == 6, 0, z)))
    M = np.zeros((8, 16), np.int64); M[1] = 4080; M[7] = 4080; M[2, 15] = 4080; M[3, 0] = 4080; M[4, ::2] = 4080; M[5, :15] = 4080
    mode = (np.arange(N)[:, None] + np.arange(8)) % 8
    t = np.where((mode == 6)[:, :, None, None], rng.choice(np.array([0, 1, 4079, 4080, 1300]), t.shape), M[mode][..., None])
    q = rng.permutation(N); t[q[0]] = 0; t[q[1]] = 4080
    a = rng.integers(0, 3, (N, 8, 1, 1)); a[:, 0] = 0; a[:, 7] = 1; w = np.where(a == 0, 0, np.where(a == 1, 63, w))
    W = np.where(rng.random((N, 8, 1, 1)) < 0.4, (VX - 1) * rng.integers(0, 2, W.shape), W)
    G = np.where(rng.random((N, 8, 1, 1)) < 0.4, (VY - 1) * rng.integers(0, 2, G.shape), G)
    z[q[1], ::2] = 0
    e = int(q[2])
    X[e] = np.minimum(X[e], 254); Y[e] = rng.integers(0, 61, Y[e].shape); K[e] = rng.integers(0, h, K[e].shape); z[e] = 255; t[e] = rng.integers(2900, 3301, t[e].shape)
    b = int(q[3]); gb = (7 - b) % 8
    X[b, gb] = np.minimum(X[b, gb], 254); z[b, gb] = 255
    return pack(X, Y, K, G, W, z, w, t)
def setup_inputs_ties(rng):
    X, Y, K, G, W, z, w, t = parts(rng)
    X[:, ::2] = 128 * rng.integers(0, 2, (N, 4, 16, VX)); Y[:, ::2] = 128 * rng.integers(0, 2, (N, 4, 16, VY))
    X[:, 1::2] = 85 * rng.integers(0, 4, (N, 4, 16, VX)); Y[:, 1::2] = 85 * rng.integers(0, 4, (N, 4, 16, VY))
    z[:, ::2] = 16 * rng.integers(0, 9, (N, 4, 16, C)); z[:, 1::2] = np.maximum(85 * rng.integers(0, 4, (N, 4, 16, C)) - 16 * rng.integers(0, 8, (N, 4, 16, C)), 0)
    t[:, ::2] = 128 * rng.integers(6, 12, (N, 4, 16, 1)); t[:, 1::2] = 85 * rng.integers(17, 24, (N, 4, 16, 1))
    t = t + rng.integers(-1, 2, t.shape) * (rng.random(t.shape) < 0.5)
    X[:, 5] = rng.integers(200, 256, (N, 16, VX)); Y[:, 5] = rng.integers(0, 61, (N, 16, VY))
    X[:, 6] = rng.integers(0, 61, (N, 16, VX)); Y[:, 6] = rng.integers(200, 256, (N, 16, VY))
    t[:, 5:7] = 3160 + rng.integers(-300, 151, (N, 2, 16, 1))
    return pack(X, Y, K, G, W, z, w, t)
def setup_inputs_alike(rng):
    X, Y, K, G, W, z, w, t = parts(rng)
    K[:, ::2] = K[:, ::2, :1, :].copy(); K[:, 1] = K[:, 1, :, :1].copy(); W[:, 1] = W[:, 1, :, :1].copy()
    W[:, 2:4] = np.repeat(K[:, 2:4], B, axis=-1); G[:, 4] = G[:, 4, :1, :1].copy(); z[:, 5] = z[:, 5, :, :1].copy()
    few = np.array([0, VX - 1, VX // 2, 3]); K[:, 7] = rng.choice(few, (N, 16, C)); W[:, 7] = rng.choice(few, (N, 16, B * C))
    return pack(X, Y, K, G, W, z, w, t)
def check_inputs(d):
    bad = []
    for k, hi in (("gx", 255), ("sy", 255), ("rk", VX - 1), ("rt", VY - 1), ("wr", VX - 1), ("z0", 255), ("wt", 63), ("th", 4080)):
        a = np.asarray(d[k]).astype(np.float64)
        if not (np.min(a) >= 0 and np.max(a) <= hi): bad.append("range of " + k)
        elif not np.all(a == np.floor(a)): bad.append("whole numbers of " + k)
    return bad
def reference(gx, sy, rk, rt, wr, z0, wt, th):
    ints = lambda a, n: a.astype(np.float32).astype(np.int32).reshape(N, 8, 16, n)
    X, Y, z, w = ints(gx, VX), ints(sy, VY), ints(z0, C), ints(wt, 1)
    K = rk.astype(np.int64).reshape(N, 8, 16, C); G = rt.astype(np.int64).reshape(N, 8, 16, B * C); W = wr.astype(np.int64).reshape(N, 8, 16, B * C)
    t = th.astype(np.int64).reshape(N, 8, 16, 1); A = np.zeros((N, 1, 1, 1), np.int64)
    margin = (16 * ((15 - np.arange(16)) >> 1)).astype(np.int32)[:, None]
    for lead in range(LE):
        if lead > 0: K = np.roll(K, 1, axis=0); z = np.roll(z, 1, axis=0)
        u = np.add.reduce(w.astype(np.int64) * z, axis=2) & 4095
        c = B * np.arange(C) + (((u * u) >> 5) & (B - 1)); cc = np.broadcast_to(c[:, :, None, :], K.shape)
        route = np.take_along_axis(G, cc, 3); old = np.take_along_axis(W, cc, 3)
        s = (((route * K) >> 5) + route + 37 * u[:, :, None, :]) & (VY - 1)
        x = np.take_along_axis(X, K.reshape(N, 8, 1, 16 * C), 3).reshape(N, 8, 16, 16, C)
        y = np.take_along_axis(Y, s.reshape(N, 8, 1, 16 * C), 3).reshape(N, 8, 16, 16, C)
        placed = np.add.reduce(np.abs(x - y), axis=2) < t + A
        hold = placed & (np.count_nonzero(x >= z[:, :, :, None, :] + margin, axis=2) >= 9)
        stop = np.logical_or.accumulate(hold[:, :, ::-1], axis=2)[:, :, ::-1]
        held = placed & stop; fail = placed & ~stop
        h, f, o = held.astype(np.int64), fail.astype(np.int64), 1 - placed.astype(np.int64)
        nh = np.add.reduce(h, axis=2)[:, :, None]; nf = np.add.reduce(f, axis=2)[:, :, None]
        over = np.add.accumulate(h[:, :, ::-1], axis=2)[:, :, ::-1] - h
        pos = np.where(held, over, np.where(fail, nh + np.add.accumulate(f, axis=2) - f, nh + nf + np.add.accumulate(o, axis=2) - o))
        new = np.zeros_like(K); np.put_along_axis(new, pos, np.where(fail, old, K), 2)
        np.put_along_axis(W, cc, np.where(fail, K, old), 3)
        z = np.abs(z - np.maximum.reduce(np.where(held[:, :, None], x, 0), axis=3))
        A = 16 * (np.add.reduce(f, axis=(1, 2, 3)) & 31).reshape(N, 1, 1, 1)
        K = new
    return {"yk": K.reshape(N, 128, C).astype(np.float32), "yw": W.reshape(N, 128, B * C).astype(np.float32), "yz": z.reshape(N, 128, C).astype(np.float32).astype(BF)}

from concourse.bass import DstId, RemoteDMATransfer
from concourse.mybir import dt, AluOpType as OP, AxisListType, ActivationFunctionType as AF

VX, VY, C, LE = 2048, 4096, 256, 5
NCH = 2
n = C // NCH
SB = 64
NS_ = n // SB
nq = n // 16
PAD = 32
KB = 512 // n
NB = 16 // KB
ABS_S = (0,)
CFG = {"fix": {"V": 0.03, "S": 0.05, "P": 0.0, "G": 0.05, "D": 0.06, "E": 0.06}, "pe": 0.417e-3, "cy": 0.83e-3 * 1.25, "ga": 1.56,
       "sc": 3.8, "wake": 0.08, "net": 2.6, "jit": 0.0}


UF = 256
FB = 4 * ((NCH - 1) % 2)
CUR = {"lc": (0, 0)}
CACHE = {}
BIAS = {("UL", 0): -17.0, ("x", 0): 5.0, ("xz", 0): -1.9, ("sg", 0): 15.0, ("cnt", 0): -12.2, ("y", 0): 40.4, ("abs", 0): -0.9, ("D", 0): 14.1, ("relu", 0): 39.5,
        ("mk", 0): 6.4, ("wg", 0): 8.4, ("dk", 0): -4.9, ("va", 0): -20.3, ("E", 0): 7.3, ("xh", 0): -24.3, ("scan", 0): -0.8, ("clamp", 0): 0.6, ("NM", 0): -24.8,
        ("scat", 0): 17.4, ("K'", 0): -3.6, ("UL", 1): 1.8, ("D", 1): -5.6, ("scan", 1): -10.1, ("R", 1): 3.3, ("relu", 1): -7.6, ("scat", 1): 1.1, ("E", 1): -7.5,
        ("va", 1): -1.1, ("z'", 1): 10.5, ("fd", 1): -11.2, ("P", 1): 16.2, ("cd", 1): 3.7, ("K'", 1): 8.0, ("NM", 1): 0.5, ("abs", 1): -6.7, ("cnt", 1): -2.0,
        ("dk", 1): -7.1, ("sg", 1): 6.2, ("wg", 1): -1.7, ("x", 1): -6.6, ("xz", 1): 6.9}


def two(name, dtype, cols):
    return {name: ("sbuf", [128, cols], dtype)}


SCRATCH = {}
for _nm, _dt, _co in (
        ("gearb", "bfloat16", PAD + VX), ("siteb", "bfloat16", VY), ("rkb", "int32", C), ("rtb", "int32", 2 * C), ("wri", "int32", 2 * C),
        ("wrb", "float32", 2 * C), ("wtb", "bfloat16", 2), ("thb", "int32", 2), ("tcol", "float32", 2), ("tac", "float32", 8),
        ("lst", "uint16", LE * C), ("lsend", "uint16", LE * C), ("zb", "bfloat16", LE * C), ("zsend", "bfloat16", LE * C),
        ("ci", "int32", 2 * NCH * nq), ("v5", "int32", 2 * NCH * nq), ("vv", "int32", 2 * NCH * nq), ("bi", "int32", 2 * NCH * nq),
        ("cc", "int32", 2 * NCH * nq), ("cl", "uint16", 2 * C),
        ("k32", "float32", 2 * C), ("k16", "float16", 2 * C), ("pp", "int32", 2 * C), ("qq", "int32", 2 * C), ("tt", "int32", 2 * C),
        ("t2", "int32", 2 * C), ("sl", "uint16", 2 * C),
        ("xx", "bfloat16", 32 * C), ("dd", "bfloat16", 32 * C), ("da", "bfloat16", 32 * C), ("sg", "bfloat16", 32 * C),
        ("pm", "bfloat16", 2 * C), ("hd", "bfloat16", 2 * C), ("ff", "bfloat16", 2 * C), ("mk", "float32", 2 * C), ("hl", "uint16", 2 * C),
        ("xh", "bfloat16", 32 * C), ("xs", "bfloat16", 32 * C), ("rr", "bfloat16", 4 * C), ("po", "bfloat16", 2 * C),
        ("wg", "float32", 2 * C), ("dk", "float32", 2 * C), ("fd", "float32", 2 * C), ("va", "float16", 2 * C), ("kl", "float16", 32 * C),
        ("yks", "float32", C), ("yws", "float32", 2 * C),
        ("fs", "bfloat16", LE * NCH), ("fi", "int32", LE), ("fm", "int32", LE),
        ("one", "bfloat16", 2048), ("b1", "bfloat16", 144), ("b2", "bfloat16", 144), ("bn", "bfloat16", 144), ("bh", "bfloat16", 144),
        ("bw", "bfloat16", 144), ("tmpa", "bfloat16", 144), ("tmpb", "bfloat16", 144), ("tmpc", "bfloat16", 128),
        ("blk", "bfloat16", 128), ("idn", "bfloat16", 128), ("idm", "bfloat16", 128), ("i16", "bfloat16", 128), ("i20", "bfloat16", 128),
        ("i64", "bfloat16", 128), ("im64", "bfloat16", 128), ("i384", "bfloat16", 128),
        ("tri", "bfloat16", 128), ("tri4", "bfloat16", 128), ("low", "bfloat16", 128), ("upp", "bfloat16", 128), ("upm", "bfloat16", 128),
        ("bk", "bfloat16", 2048), ("bp", "bfloat16", 2048), ("mb0", "bfloat16", 128), ("mb1", "bfloat16", 128),
        ("w37", "float32", 2), ("wa", "bfloat16", 2), ("wb", "float32", 2), ("wac", "float32", 2), ("wcol", "float32", 2),
        ("lwa", "bfloat16", 128), ("lwb", "bfloat16", 128),
        ("rst", "bfloat16", 16 * n), ("io2", "int32", nq), ("kf", "float32", 2), ("cz", "float32", 8),
        ("c64", "float32", 2), ("c15", "float32", 2), ("cnm", "float32", 2), ("cny", "float32", 2)):
    SCRATCH.update(two(_nm, _dt, _co))
for _b in range(8):
    SCRATCH["ps%d" % _b] = ("psum", [128, 512], "float32")

LOADS = ("gear", "site", "rk", "rt", "wr", "z", "wt", "th")
SEMAPHORES = ["sV", "sS", "sP", "sG", "sent"] + ["ld_" + x for x in LOADS] + ["st%d" % i for i in range(3 * NCH)]
SEMAPHORES += ["a%s%d_%d" % (k, e, c) for k in "kz" for e in range(1, LE) for c in range(NCH)]


def sl(T, name, a, b, st=1):
    return T[name][:, a:b] if st == 1 else T[name][:, a:b:st]


def build():
    ops = []
    cy, ga, fix = CFG["cy"], CFG["ga"], CFG["fix"]

    def add(eng, cost, fn, rd=(), wr=(), bank=(), name="", lat=0.0, sem=None, inc=1, acc=None):
        ops.append({"e": eng, "dur": cost + fix[eng], "fn": fn, "rd": list(rd), "wr": list(wr), "bank": list(bank), "name": name,
                    "lat": lat, "sem": sem, "inc": inc, "lc": CUR["lc"], "acc": acc})

    def vcost(m, cyc=1.0):
        return max(64, m * cyc) * cy

    def gcost(m):
        return 0.04 + m * ga * cy

    def pcost(*cols):
        return sum(max(64, x) for x in cols) * CFG["pe"] * 1.25

    def load(q, dst, src, a, b, key, lat):
        add(q, 0.0, lambda g, T, e: e.dma_start(sl(T, dst, a, b), T[src][:]), wr=[dst] if dst != "zb" else [("zb", 0, c) for c in range(NCH)],
            name="load " + src, lat=lat, sem="ld_" + key, inc=16)
    load("D", "wtb", "wt", 0, 1, "wt", 2.0)
    load("E", "zb", "z0", 0, C, "z", 2.0)
    load("D", "rkb", "rk", 0, C, "rk", 2.2)
    load("D", "gearb", "gx", PAD, PAD + VX, "gear", 4.5)
    load("E", "rtb", "rt", 0, 2 * C, "rt", 3.5)
    load("E", "thb", "th", 0, 1, "th", 4.0)
    load("D", "siteb", "sy", 0, VY, "site", 8.0)
    load("E", "wri", "wr", 0, 2 * C, "wr", 4.0)

    def aff(dst, src, m, pat, cmp_, base, cm, w=None):
        add("G", 0.17 + 2 * m * cy, lambda g, T, e: e.affine_select(sl(T, dst, 0, m), sl(T, src, 0, m), pat, cmp_, 0.0, base, cm),
            rd=[src], wr=[dst], name="aff " + dst)

    def iot(dst, m, pat, base, cm):
        def f(g, T, e):
            if SCRATCH[dst][2] == "int32":
                return e.iota(sl(T, dst, 0, m), pat, base, cm)
            return e.iota(sl(T, dst, 0, m), pat, base, cm, allow_small_or_imprecise_dtypes=True)
        add("G", 0.13 + 2 * m * cy, f, wr=[dst], name="iota " + dst)

    def ts(dst, a, b, src, c0, d, s1, s2, o1, o2=None, rd=None, wr=None, cyc=1.0, bank=(), eng="V", st=1, sst=1, dst_st=1):
        def f(g, T, e):
            x1 = s1(T) if callable_(s1) else s1
            x2 = s2(T) if callable_(s2) else s2
            if o2 is None:
                return e.tensor_scalar(sl(T, dst, a, b, dst_st), sl(T, src, c0, d, sst), x1, None, o1)
            return e.tensor_scalar(sl(T, dst, a, b, dst_st), sl(T, src, c0, d, sst), x1, x2, o1, o2)
        add("V", vcost((b - a) // dst_st, cyc), f, rd=rd, wr=wr, bank=bank, name="ts " + dst)

    def callable_(x):
        return not isinstance(x, (int, float)) and x is not None

    def cst(dst, src, m, mul, addv=None):
        if addv is None:
            ts(dst, 0, m, src, 0, m, mul, None, OP.mult, rd=[src], wr=[dst], cyc=0.5)
        else:
            ts(dst, 0, m, src, 0, m, mul, addv, OP.mult, OP.add, rd=[src], wr=[dst])

    add("V", 0.3, lambda g, T, e: e.memset(T.one[:, 0:144], 1.0), wr=["one"], name="one")
    add("V", vcost(32), lambda g, T, e: e.memset(T.gearb[:, 0:PAD], 0.0), wr=["gpad"], name="gpad")
    aff("tmpa", "one", 144, [[-16, 9], [0, 16]], OP.is_ge, 0, 1)
    aff("tmpb", "tmpa", 144, [[16, 9], [0, 16]], OP.is_ge, 15, -1)
    aff("b1", "tmpb", 144, [[0, 9], [1, 16]], OP.is_equal, -15, 0)
    ts("wcol", 0, 1, "wtb", 0, 1, 1.0, None, OP.mult, rd=["wtb"], wr=["wcol"])
    add("V", vcost(144, .5), lambda g, T, e: e.tensor_scalar(T.bw[:, 0:144], T.b1[:, 0:144], T.wcol[:, 0:1], None, OP.mult), rd=["b1", "wcol"], wr=["bw"], name="bw")
    iot("io2", nq, [[32, nq]], 0, 0)
    iot("kf", 1, [[0, 1]], 0, 1)
    ts("w37", 0, 1, "wtb", 0, 1, 37.0, None, OP.mult, rd=["wtb"], wr=["w37"])
    ts("wa", 0, 1, "w37", 0, 1, 1.0, None, OP.mult, rd=["w37"], wr=["wa"])
    ts("wac", 0, 1, "wa", 0, 1, 1.0, None, OP.mult, rd=["wa"], wr=["wac"])
    add("V", vcost(1), lambda g, T, e: e.tensor_tensor(T.wb[:, 0:1], T.w37[:, 0:1], T.wac[:, 0:1], OP.subtract), rd=["w37", "wac"], wr=["wb"], name="wb")
    add("V", vcost(128, .5), lambda g, T, e: e.tensor_scalar(T.lwa[:, 0:128], T.tmpb[:, 0:128], T.wac[:, 0:1], None, OP.mult), rd=["tmpb", "wac"], wr=["lwa"], name="lwa")
    add("V", vcost(128, .5), lambda g, T, e: e.tensor_scalar(T.lwb[:, 0:128], T.tmpb[:, 0:128], T.wb[:, 0:1], None, OP.mult), rd=["tmpb", "wb"], wr=["lwb"], name="lwb")
    add("V", vcost(1), lambda g, T, e: e.tensor_copy(T.ci[:, 0:1], T.kf[:, 0:1]), rd=["kf"], wr=[("ci", 0, 0)], name="k0")
    ts("v5", 0, 1, "ci", 0, 1, 15, None, OP.bitwise_and, rd=[("ci", 0, 0)], wr=[("v5", 0, 0)])
    ts("cz", 0, 1, "v5", 0, 1, 1.0, None, OP.mult, rd=[("v5", 0, 0)], wr=["cz"])
    cst("c64", "cz", 1, 1.0, -64.0)
    cst("c15", "cz", 1, -1.0, 15.0)
    cst("cny", "cz", 1, 2048.0, -2048.0 * 15)
    cst("cnm", "cz", 1, 2048.0, -2048.0 * 15 + PAD)
    add("V", vcost(nq), lambda g, T, e: e.tensor_scalar(T.cc[:, 0:nq], T.io2[:, 0:nq], T.cz[:, 0:1], T.cz[:, 0:1], OP.add, OP.add), rd=["io2", "cz"],
        wr=[("cc", 0, 0)], name="io2b")
    add("V", vcost(nq), lambda g, T, e: e.tensor_copy(T.io2[:, 0:nq], T.cc[:, 0:nq]), rd=[("cc", 0, 0)], wr=["io2"], name="io2c")
    ts("tcol", 0, 1, "thb", 0, 1, 1.0, None, OP.mult, rd=["thb"], wr=["tcol"])
    ts("tac", 0, 1, "thb", 0, 1, 1.0, None, OP.mult, rd=["thb"], wr=[("tac", 0)])
    aff("idn", "one", 128, [[-1, 128]], OP.is_equal, 0, 1)
    cst("idm", "idn", 128, -1.0)
    cst("i16", "idn", 128, 16.0)
    cst("bh", "b1", 144, 0.5)
    cst("b2", "b1", 144, 2.0)
    cst("bn", "b1", 144, -1.0)
    aff("tri", "tmpb", 128, [[-1, 128]], OP.is_ge, 0, 1)
    cst("tri4", "tri", 128, 4096.0)
    cst("i20", "idn", 128, 1048576.0)
    aff("low", "tmpb", 128, [[1, 128]], OP.is_ge, -1, -1)
    aff("upp", "tmpb", 128, [[-1, 128]], OP.is_ge, -1, 1)
    cst("upm", "upp", 128, -1.0)
    cst("i64", "idn", 128, 64.0)
    cst("im64", "idn", 128, -64.0)
    cst("i384", "idn", 128, 3840.0)
    iot("mb0", 128, [[0, 8], [-32, 16]], 0, 0)
    add("V", vcost(128, 2), lambda g, T, e: e.tensor_tensor(T.mb1[:, 0:128], T.mb0[:, 0:128], T.tmpb[:, 0:128], OP.mult), rd=["mb0", "tmpb"], wr=["mb1"], name="mb1")
    add("V", vcost(2048, .5), lambda g, T, e: e.memset(T.kl[:, 0:16], 0) if False else e.memset(T.rst[:, 0:16 * n], 1.0), wr=["rst1"], name="rst1")
    aff_src = "rst1"
    add("G", 0.17 + 2 * 2048 * cy, lambda g, T, e: e.affine_select(T.bk[:, 0:2048], T.rst[:, 0:2048], [[-1, 16], [-16, 8], [0, 16]], OP.is_equal, 0.0, 0, 1),
        rd=[aff_src, "upp", "low", "tri", "idn"], wr=["bk"], name="bk")
    add("V", vcost(n), lambda g, T, e: e.memset(T.rst[:, 0:16 * n:16], 0.0), rd=["rst1", "bk"], wr=["rst", "rst1"], name="rst")
    for j in range(4):
        b = j + 2 if j < 2 else j + 4

        def fbp(g, T, e, j=j, b=b):
            ps = T["ps%d" % b]
            for k in range(4):
                e.matmul(ps[:, 128 * k:128 * k + 128], T.i384[:, 0:128], T.bk[:, 512 * j + 128 * k:512 * j + 128 * k + 128], True, False)
                r = e.matmul(ps[:, 128 * k:128 * k + 128], T.idn[:, 0:128], T.mb1[:, 0:128], False, True)
            return r
        add("P", pcost(*[128] * 8), fbp, rd=["i384", "bk", "idn", "mb1"], wr=[("bpp", j)], bank=[b], name="bpp")
        add("S", 512 * cy, lambda g, T, e, j=j, b=b: e.activation(T.bp[:, 512 * j:512 * j + 512], T["ps%d" % b][:, 0:512], AF.Copy), rd=[("bpp", j)], wr=["bp%d" % j],
            bank=[b], name="bp")
    BP = ["bp%d" % j for j in range(4)]
    for c in range(NCH):
        i0 = c * n
        ts("lst", i0, i0 + n, "rkb", i0, i0 + n, float(PAD), None, OP.add, rd=["rkb"], wr=[("lst", 0, c)])

    def wrprep(c):
        ts("wrb", 2 * c * n, 2 * c * n + 2 * n, "wri", 2 * c * n, 2 * c * n + 2 * n, float(PAD), None, OP.add, rd=["wri"], wr=[("wrb", c)])

    for e_ in range(LE):
        for c in range(NCH):
            CUR["lc"] = (e_, c)
            chunk(add, ts, vcost, gcost, pcost, e_, c, BP, wrprep, cy)
    return ops


def count(add, vcost, pcost, e_):
    def ff2(g, T, e):
        ps = T["ps%d" % FB]
        for c in range(NCH):
            r = e.matmul(ps[:, UF + 1:UF + 2], T.one[:, 0:128], T.fs[:, e_ * NCH + c:e_ * NCH + c + 1], c == 0, c == NCH - 1)
        return r
    add("P", pcost(*[64] * NCH), ff2, rd=["one"] + [("fs", e_, c) for c in range(NCH)], wr=[("f2", e_)], bank=[FB], name="F2")
    add("V", vcost(1), lambda g, T, e: e.tensor_copy(T.fi[:, e_:e_ + 1], T["ps%d" % FB][:, UF + 1:UF + 2]), rd=[("f2", e_)], wr=[("fi", e_)], bank=[FB], name="fi")
    add("V", vcost(1), lambda g, T, e: e.tensor_scalar(T.fm[:, e_:e_ + 1], T.fi[:, e_:e_ + 1], 31, None, OP.bitwise_and), rd=[("fi", e_)], wr=[("fm", e_)], name="fm")
    add("V", vcost(1), lambda g, T, e: e.tensor_scalar(T.tac[:, e_ + 1:e_ + 2], T.fm[:, e_:e_ + 1], 16.0, T.tcol[:, 0:1], OP.mult, OP.add),
        rd=[("fm", e_), "tcol"], wr=[("tac", e_ + 1)], name="ta")


def chunk(add, ts, vcost, gcost, pcost, e_, c, BP, wrprep, cy):
    i0 = c * n
    pr = e_ % 2
    o = pr * C + i0
    of = 16 * o
    R0, R1, X0, X1 = 4 * (c % 2), 4 * (c % 2) + 1, 4 * (c % 2) + 2, 4 * (c % 2) + 3
    lz = e_ * C + i0
    ot = (pr * NCH + c) * nq
    last = e_ == LE - 1
    t = lambda nm, *x: (nm, pr, c) + x
    L, Z = ("lst", e_, c), ("zb", e_, c)

    def mm(out, lhs, rhs, start, stop):
        return lambda T, e: e.matmul(out(T), lhs(T), rhs(T), start, stop)

    def PS(b, a, w):
        return lambda T: T["ps%d" % b][:, a:a + w]

    def M(nm, a=0, w=128):
        return lambda T: T[nm][:, a:a + w]

    def Sx(nm, a, b, st):
        return lambda T: T[nm][:, a:b:st]

    def pe(mms, cols, **kw):
        def f(g, T, e):
            for m in mms:
                r = m(T, e)
            return r
        add("P", pcost(*cols), f, **kw)

    def group(out, pairs):
        return [mm(out, l, r, i == 0, i == len(pairs) - 1) for i, (l, r) in enumerate(pairs)]

    def act(out, src, func, m, bias=None, **kw):
        def f(g, T, e):
            if bias is None:
                return e.activation(out(T), src(T), func)
            return e.activation(out(T), src(T), func, bias=bias(T) if not isinstance(bias, float) else bias)
        add("S", m * cy, f, **kw)

    def vec(f, m, cyc=1.0, cost=None, **kw):
        add("V", vcost(m, cyc) if cost is None else cost, lambda g, T, e: f(T, e), **kw)

    pe(group(PS(R0, 0, nq), [(M("bw", 15 - m), Sx("zb", lz + m, lz + n, 16)) for m in range(16)]), [64] * 16, rd=["bw", Z], wr=[t("ul")], bank=[R0], name="UL")
    vec(lambda T, e: e.tensor_copy(T.ci[:, ot:ot + nq], T["ps%d" % R0][:, 0:nq]), nq, rd=[t("ul")], wr=[t("ci")], bank=[R0], name="ci")
    vec(lambda T, e: e.tensor_scalar(T.v5[:, ot:ot + nq], T.ci[:, ot:ot + nq], 31, None, OP.bitwise_and), nq, rd=[t("ci")], wr=[t("v5")], name="v5")
    vec(lambda T, e: e.tensor_tensor(T.vv[:, ot:ot + nq], T.v5[:, ot:ot + nq], T.v5[:, ot:ot + nq], OP.mult), nq, 2, rd=[t("v5")], wr=[t("vv")], name="vv")
    vec(lambda T, e: e.tensor_scalar(T.bi[:, ot:ot + nq], T.vv[:, ot:ot + nq], 5, 1, OP.arith_shift_right, OP.bitwise_and), nq, rd=[t("vv")], wr=[t("bi")], name="bi")
    vec(lambda T, e: e.tensor_tensor(T.cc[:, ot:ot + nq], T.bi[:, ot:ot + nq], T.io2[:, 0:nq], OP.add), nq, 2, rd=[t("bi"), "io2"], wr=[t("cc")], name="cc")
    oc = (pr * NCH + c) * n
    vec(lambda T, e: e.tensor_copy(T.cl[:, oc:oc + nq], T.cc[:, ot:ot + nq]), nq, rd=[t("cc")], wr=[t("cl")], name="cl")
    pe(group(PS(R0, 128, n), [(M("lwa"), M("zb", lz, n)), (M("lwb"), M("zb", lz, n))]), [n] * 2, rd=["lwa", "lwb", Z], wr=[t("u37")], bank=[R0], name="U37")

    vec(lambda T, e: e.tensor_copy(T.k32[:, o:o + n], T.lst[:, lz:lz + n]), n, rd=[L], wr=[t("k32")], name="k32")
    for s in range(NS_):
        a = of + s * SB * 16
        add("S", gcost(SB * 16), lambda g, T, e, a=a, s=s: e.activation(T.xx[:, a:a + SB * 16], T.gearb[:, 0:PAD + VX].indirect(T.lst[:, lz + s * SB:lz + s * SB + SB]), AF.Copy),
            rd=["gearb", "gpad", L], wr=[t("xx", s)], name="x")
    vec(lambda T, e: e.tensor_tensor(T.pp[:, o:o + n], T.rtb[:, 2 * i0:2 * i0 + 2 * n].indirect(T.cl[:, oc:oc + nq]), T.k32[:, o:o + n], OP.mult), n, cost=gcost(n),
        rd=["rtb", t("cl"), t("k32")], wr=[t("pp")], name="P")
    vec(lambda T, e: e.tensor_scalar(T.qq[:, o:o + n], T.pp[:, o:o + n], 5, None, OP.arith_shift_right), n, rd=[t("pp")], wr=[t("qq")], name="Q")
    vec(lambda T, e: e.tensor_tensor(T.tt[:, o:o + n], T.qq[:, o:o + n], T["ps%d" % R0][:, 128:128 + n], OP.add), n, rd=[t("qq"), t("u37")], wr=[t("tt")], bank=[R0], name="T")
    vec(lambda T, e: e.tensor_scalar(T.t2[:, o:o + n], T.tt[:, o:o + n], 4095, None, OP.bitwise_and), n, rd=[t("tt")], wr=[t("t2")], name="T2")
    vec(lambda T, e: e.tensor_copy(T.sl[:, o:o + n], T.t2[:, o:o + n]), n, rd=[t("t2")], wr=[t("sl")], name="SL")

    for j in range(NB):
        b = (X0, X1)[j % 2]
        ms, cols = [], []
        for kk in range(KB):
            k = j * KB + kk
            ms += group(PS(b, kk * n, n), [(M("idn"), Sx("xx", of + k, of + 16 * n, 16)), (M("idm"), M("zb", lz, n))])
            cols += [n, n]
        pe(ms, cols, rd=["idn", "idm", Z] + [t("xx", s) for s in range(NS_)], wr=[t("xz", j)], bank=[b], name="xz")
        for h in range(KB // 2):
            k = j * KB + 2 * h
            bias = 0.5 - 16 * ((15 - k) // 2)
            add("S", 2 * n * cy, lambda g, T, e, b=b, h=h, k=k, v=k // 2: e.activation(T.sg[:, of + k * n:of + k * n + 2 * n], T["ps%d" % b][:, 2 * h * n:2 * h * n + 2 * n],
                AF.Sign, bias=T.mcol[:, v:v + 1] if False else 0.5 - 16 * ((15 - k) // 2)), rd=[t("xz", j)], wr=[t("sg", k // 2)], bank=[b], name="sg")
        pe([mm(PS(R1, 0, n), M("bh", 15 - k), M("sg", of + k * n, n), k == 0, False) for k in range(j * KB, j * KB + KB)], [n] * KB,
           rd=["bh"] + [t("sg", v) for v in range(j * KB // 2, j * KB // 2 + KB // 2)], wr=[t("cn", j)], bank=[R1], acc=("cn", e_, c), name="cnt")

    for s in range(NS_):
        a = of + s * SB * 16
        w = SB * 16
        vec(lambda T, e, a=a, w=w, s=s: e.tensor_tensor(T.dd[:, a:a + w], T.siteb[:, 0:VY].indirect(T.sl[:, o + s * SB:o + s * SB + SB]), T.xx[:, a:a + w], OP.subtract), w, cost=gcost(w),
            rd=["siteb", t("sl"), t("xx", s)], wr=[t("dd", s)], name="y")
        ab = s in ABS_S
        if ab:
            act(M("da", a, w), M("dd", a, w), AF.Abs, w, rd=[t("dd", s)], wr=[t("da", s)], name="abs")
            pairs = [(M("b1", 15 - k), Sx("da", a + k, a + w, 16)) for k in range(16)]
        else:
            vec(lambda T, e, a=a, w=w: e.tensor_scalar(T.da[:, a:a + w], T.dd[:, a:a + w], 0.0, None, OP.max), w, 0.5, rd=[t("dd", s)], wr=[t("da", s)], name="relu")
            pairs = [(M("bn", 15 - k), Sx("dd", a + k, a + w, 16)) for k in range(16)] + [(M("b2", 15 - k), Sx("da", a + k, a + w, 16)) for k in range(16)]
        if ab:
            pe(group(PS(R0, 256 + s * SB, SB), pairs), [SB] * len(pairs), rd=["b1", t("da", s)], wr=[t("D", s)], bank=[R0], name="D")
        else:
            pe(group(PS(R0, 256 + s * SB, SB), pairs), [SB] * len(pairs), rd=["b2", "bn", t("dd", s), t("da", s)], wr=[t("D", s)], bank=[R0], name="D")
    vec(lambda T, e: e.tensor_scalar(T.pm[:, o:o + n], T["ps%d" % R0][:, 256:256 + n], T.tac[:, e_:e_ + 1], -1.0, OP.is_lt, OP.add), n,
        rd=[t("D", s) for s in range(NS_)] + [("tac", e_)], wr=[t("pm")], bank=[R0], name="p")
    pe([mm(PS(R1, 0, n), M("i16"), M("pm", o, n), False, True)], [n], rd=["i16", t("pm")], wr=[t("cn")], bank=[R1], acc=("cn", e_, c), name="cnp")
    act(M("hd", o, n), PS(R1, 0, n), AF.Relu, n, rd=[t("cn")], wr=[t("hd")], bank=[R1], name="hold")
    pe(group(PS(R1, 128, n), [(M("i20"), M("pm", o, n)), (M("tri4"), M("hd", o, n))]), [n] * 2, rd=["tri4", "i20", t("hd"), t("pm")], wr=[t("H")], bank=[R1], name="H")
    vec(lambda T, e: e.tensor_scalar(T.ff[:, o:o + n], T["ps%d" % R1][:, 128:128 + n], 0.0, None, OP.is_equal), n, rd=[t("H")], wr=[t("ff")], bank=[R1], name="f")
    vec(lambda T, e: e.tensor_tensor(T.mk[:, o:o + n], T.k32[:, o:o + n], T["ps%d" % R1][:, 128:128 + n], OP.min), n, rd=[t("H"), t("k32")], wr=[t("mk")], bank=[R1], name="mk")
    vec(lambda T, e: e.tensor_copy(T.hl[:, o:o + n], T.mk[:, o:o + n]), n, rd=[t("mk")], wr=[t("hl")], name="hl")
    if e_ == 0:
        wrprep(c)
    vec(lambda T, e: e.tensor_scalar(T.k16[:, o:o + n], T.lst[:, lz:lz + n], -float(PAD), None, OP.add), n, 0.5, rd=[L], wr=[t("k16")], name="k16")
    add("S", gcost(n), lambda g, T, e: e.activation(T.wg[:, o:o + n], T.wrb[:, 2 * i0:2 * i0 + 2 * n].indirect(T.cl[:, oc:oc + nq]), AF.Copy), rd=[("wrb", c), t("cl")], wr=[t("wg")],
        name="wg")
    vec(lambda T, e: e.tensor_tensor(T.dk[:, o:o + n], T.wrb[:, 2 * i0:2 * i0 + 2 * n].indirect(T.cl[:, oc:oc + nq]), T.k32[:, o:o + n], OP.subtract), n, cost=gcost(n),
        rd=[("wrb", c), t("cl"), t("k32")], wr=[t("dk")], name="dk")
    vec(lambda T, e: e.tensor_tensor(T.fd[:, o:o + n], T.dk[:, o:o + n], T.ff[:, o:o + n], OP.mult), n, 2, rd=[t("dk"), t("ff")], wr=[t("fd")], name="fd")
    vec(lambda T, e: e.tensor_tensor(T.va[:, o:o + n], T.k16[:, o:o + n], T.fd[:, o:o + n], OP.add), n, 2, rd=[t("k16"), t("fd")], wr=[t("va")], name="va")
    pe(group(PS(R0, 0, n), [(M("low"), M("pm", o, n)), (M("i64"), M("ff", o, n))]) + group(PS(R0, n, n), [(M("im64"), M("pm", o, n)), (M("upp"), M("ff", o, n))]),
       [n] * 4, rd=["low", "i64", "im64", "upp", t("pm"), t("ff")], wr=[t("E")], bank=[R0], name="E")
    if not last:
        pe([mm(lambda T: T["ps%d" % R0][0:n, UF:UF + 1], M("ff", o, n), M("one", 0, 1), True, True)], [64], rd=["one", t("ff")], wr=[t("fp")], bank=[R0], name="F1")
        act(lambda T: T.fs[0:n, e_ * NCH + c:e_ * NCH + c + 1], lambda T: T["ps%d" % R0][0:n, UF:UF + 1], AF.Copy, 1, rd=[t("fp")], wr=[("fs", e_, c)], bank=[R0], name="fs")
        if c == NCH - 1:
            count(add, vcost, pcost, e_)
    act(M("rr", 2 * o, 2 * n), PS(R0, 0, 2 * n), AF.Relu, 2 * n, bias=lambda T: T.c64[:, 0:1], rd=[t("E"), "c64"], wr=[t("rr")], bank=[R0], name="R")
    pe(group(PS(R0, 256, n), [(M("upp"), M("pm", o, n)), (M("upm"), M("ff", o, n)), (M("idn"), M("rr", 2 * o, n)), (M("idn"), M("rr", 2 * o + n, n))]),
       [n] * 4, rd=["upp", "upm", "idn", t("pm"), t("ff"), t("rr")], wr=[t("po0")], bank=[R0], name="POS")
    act(M("po", o, n), PS(R0, 256, n), AF.Identity, n, bias=lambda T: T.c15[:, 0:1], rd=[t("po0"), "c15"], wr=[t("po")], bank=[R0], name="po")
    for s in range(NS_):
        a = of + s * SB * 16
        w = SB * 16
        add("S", gcost(w), lambda g, T, e, a=a, w=w, s=s: e.activation(T.xh[:, a:a + w], T.gearb[:, 0:PAD + VX].indirect(T.hl[:, o + s * SB:o + s * SB + SB]), AF.Copy),
            rd=["gearb", "gpad", t("hl")], wr=[t("xh", s)], name="xh")
        vec(lambda T, e, a=a, w=w: e.tensor_tensor_scan(T.xs[:, a:a + w], T.rst[:, 0:w], T.xh[:, a:a + w], 0.0, OP.mult, OP.max), w, 0.5, rd=["rst", t("xh", s)], wr=[t("xs", s)], name="scan")
    pe(group(PS(R0, 384, n), [(M("idn"), M("zb", lz, n)), (M("idm"), Sx("xs", of + 15, of + 16 * n, 16))]), [n] * 2, rd=["idn", "idm", Z] + [t("xs", s) for s in range(NS_)],
       wr=[t("zn")], bank=[R0], name="ZN")
    zo = e_ * C + i0
    act(M("zsend", zo, n), PS(R0, 384, n), AF.Abs, n, rd=[t("zn")], wr=[("zsend", e_, c)], bank=[R0], name="z'")
    for j in range(NB):
        b = (X0, X1)[j % 2]
        ms, cols = [], []
        for kk in range(KB):
            k = j * KB + kk
            ms += group(PS(b, kk * n, n), [(M("bp", 128 * k), M("po", o, n)), (M("bk", 128 * k), M("va", o, n))])
            cols += [n, n]
        pe(ms, cols, rd=BP + ["bk", t("po"), t("va")], wr=[t("cd", j)], bank=[b], name="cd")
        a = of + j * 512
        vec(lambda T, e, a=a, b=b: e.tensor_scalar(T.kl[:, a:a + 512], T["ps%d" % b][:, 0:512], 0.0, 2048.0, OP.max, OP.min), 512, rd=[t("cd", j)], wr=[t("kl", j)], bank=[b], name="clamp")
        pe([mm(PS(R1, 256, n), M("idn"), M("kl", of + k * n, n), k == 0, k == 15) for k in range(j * KB, j * KB + KB)], [n] * KB, rd=["idn", t("kl", j)],
           wr=[t("nm") if j == NB - 1 else t("nm", j)], bank=[R1], acc=("nm", e_, c), name="NM")
    vec(lambda T, e: e.tensor_tensor(T.wrb[:, 2 * i0:2 * i0 + 2 * n].indirect(T.cl[:, oc:oc + nq]), T.wg[:, o:o + n], T.fd[:, o:o + n], OP.subtract), n, cost=0.05 + n * CFG["sc"] * cy,
        rd=[t("cl"), t("wg"), t("fd")], wr=[("wrb", c)], name="scat")
    if not last:
        vec(lambda T, e: e.tensor_scalar(T.lsend[:, zo:zo + n], T["ps%d" % R1][:, 256:256 + n], T.cnm[:, 0:1], None, OP.add), n, rd=[t("nm"), "cnm"], wr=[("lsend", e_, c)],
            bank=[R1], name="K'")
        for kind, src, dst in (("z", "zsend", "zb"), ("k", "lsend", "lst")):
            add("G", 0.3, lambda g, T, e, src=src, dst=dst, kind=kind: (g, T[dst][:, zo + C:zo + C + n], T[src][:, zo:zo + n], "a%s%d_%d" % (kind, e_ + 1, c)),
                rd=[(src, e_, c)], wr=[(dst, e_ + 1, c)], name="send" + kind, lat=CFG["net"], sem="a%s%d_%d" % (kind, e_ + 1, c), inc="net")
    else:
        vec(lambda T, e: e.tensor_scalar(T.yks[:, i0:i0 + n], T["ps%d" % R1][:, 256:256 + n], T.cny[:, 0:1], None, OP.add), n, rd=[t("nm"), "cny"], wr=[("yks", c)],
            bank=[R1], name="yk")
        act(M("yws", 2 * i0, 2 * n), M("wrb", 2 * i0, 2 * n), AF.Copy, 2 * n, bias=-float(PAD), rd=[("wrb", c)], wr=[("yws", c)], name="yw")
        for q, (dst, src, tok, a, b, sa) in enumerate((("yz", "zsend", ("zsend", e_, c), i0, i0 + n, zo), ("yw", "yws", ("yws", c), 2 * i0, 2 * i0 + 2 * n, 2 * i0),
                                                 ("yk", "yks", ("yks", c), i0, i0 + n, i0))):
            add("D", 0.0, lambda g, T, e, dst=dst, src=src, a=a, b=b, sa=sa: e.dma_start(T[dst][:, a:b], T[src][:, sa:sa + b - a]), rd=[tok], wr=[(dst, c)], name="store " + dst, lat=2.0,
                sem="st%d" % (3 * c + q), inc=16)


def depend(ops):
    wrote, readers, banks, last = {}, {}, {}, {}
    for i, op in enumerate(ops):
        d = set()
        for k in op["rd"]:
            if k in wrote:
                d.add(wrote[k])
        for k in op["wr"]:
            if k in wrote:
                d.add(wrote[k])
            d |= readers.get(k, set())
        for b in op["bank"]:
            h = banks.setdefault(b, [])
            for j in h[-40:]:
                if ops[j]["e"] != op["e"]:
                    d.add(j)
            h.append(i)
        for k in op["rd"]:
            readers.setdefault(k, set()).add(i)
        for k in op["wr"]:
            wrote[k] = i
            readers[k] = set()
        d.discard(i)
        op["dep"] = d
        op["ord"] = set()
        if op["acc"] is not None:
            if op["acc"] in last:
                op["ord"].add(last[op["acc"]])
                d.discard(last[op["acc"]])
            last[op["acc"]] = i


def order(ops):
    N_ = len(ops)
    succ = [[] for _ in range(N_)]
    for i, op in enumerate(ops):
        for j in op["dep"] | op["ord"]:
            succ[j].append(i)
    prio = [0.0] * N_
    for i in range(N_ - 1, -1, -1):
        prio[i] = ops[i]["dur"] + ops[i]["lat"] + max([prio[j] + CFG["wake"] for j in succ[i]] or [0.0])
    for i in range(N_):
        prio[i] += BIAS.get((ops[i]["name"], ops[i]["lc"][1]), 0.0)
    free, done, left = {}, [0.0] * N_, [len(op["dep"] | op["ord"]) for op in ops]
    phys = {"E": "S"}
    ready = {}
    rt = [0.0] * N_
    for i in range(N_):
        if left[i] == 0:
            ready.setdefault(phys.get(ops[i]["e"], ops[i]["e"]), []).append(i)
    seq = []
    while len(seq) < N_:
        best = None
        for q, lst in ready.items():
            if not lst:
                continue
            f = free.get(q, 0.0)
            m = min(max(f, rt[i]) for i in lst)
            if best is None or m < best[0]:
                best = (m, q)
        m, q = best
        cand = [i for i in ready[q] if max(free.get(q, 0.0), rt[i]) <= m + 1e-9]
        i = max(cand, key=lambda x: prio[x])
        ready[q].remove(i)
        op = ops[i]
        end = m + op["dur"]
        free[q] = end
        op["start"] = m
        done[i] = end + op["lat"]
        seq.append(i)
        for j in succ[i]:
            left[j] -= 1
            rt[j] = max(rt[j], done[i] + CFG["wake"])
            if left[j] == 0:
                ready.setdefault(phys.get(ops[j]["e"], ops[j]["e"]), []).append(j)
    return seq, max(done)


def plan():
    if "p" not in CACHE:
        ops = build()
        depend(ops)
        seq, span = order(ops)
        cnt = {}
        know = {}
        clock = {}
        steps = []
        for i in seq:
            op = ops[i]
            q = {"E": "S"}.get(op["e"], op["e"])
            kn = know.setdefault(q, {})
            waits = {}
            for j in sorted(op["dep"], key=lambda x: -ops[x]["pos"]):
                s, v = ops[j]["at"]
                if kn.get(s, 0) < v:
                    waits[s] = max(waits.get(s, 0), v)
                    for s2, v2 in clock[j].items():
                        kn[s2] = max(kn.get(s2, 0), v2)
            op["pos"] = len(steps)
            if op["sem"] is None:
                s = {"V": "sV", "S": "sS", "P": "sP", "G": "sG"}[op["e"]]
                cnt[s] = cnt.get(s, 0) + 1
                op["at"] = (s, cnt[s])
            else:
                op["at"] = (op["sem"], op["inc"] if op["inc"] != "net" else 1)
            clock[i] = dict(kn) if op["inc"] != "net" else {}
            clock[i][op["at"][0]] = op["at"][1]
            steps.append((op, sorted(waits.items())))
        CACHE["p"] = (steps, cnt, span)
    return CACHE["p"]


def rank_program(g, core, T, topo):
    rank = T.rank_of(core)
    if rank is None:
        return
    nxt = T.cores[(rank + 1) % len(T.cores)]
    prv = T.cores[(rank - 1) % len(T.cores)]
    rid, pid, _se = topo.addr(nxt)
    eng = topo.engines(core, nxt)[:8]
    neng_in = len(topo.engines(prv, core)[:8])
    emask = 0
    for x in eng:
        emask |= 1 << x
    queues = {"V": g.vector, "S": g.scalar, "P": g.tensor, "G": g, "D": g.sync, "E": g.scalar}
    steps, cnt, span = plan()
    sent = 0
    for op, waits in steps:
        q = queues[op["e"]]
        for s, v in waits:
            q.wait_ge(T.sem[s], neng_in if s[0] == "a" else v)
        if op["inc"] == "net":
            _g, out, in_, rs = op["fn"](g, T, q)
            g.remote_dma(out, in_, T.sem[rs], T.sem.sent, pid, rid, emask)
            sent += len(eng)
        else:
            r = op["fn"](g, T, q)
            if op["sem"] is None:
                r.then_inc(T.sem[op["at"][0]], 1)
            else:
                r.then_inc(T.sem[op["sem"]], 16)
    for s, v in sorted(cnt.items()):
        g.wait_ge(T.sem[s], v)
    g.wait_ge(T.sem.sent, sent)
    for k in LOADS:
        g.wait_ge(T.sem["ld_" + k], 16)
    for k in range(3 * NCH):
        g.wait_ge(T.sem["st%d" % k], 16)
